import numpy as np
import ml_dtypes


def mxq(x, axis, fmt="e4m3"):
    dtype, down = {"e4m3": (ml_dtypes.float8_e4m3fn, 7), "e5m2": (ml_dtypes.float8_e5m2, 14)}[fmt]
    v = np.moveaxis(np.asarray(x, np.float32).astype(ml_dtypes.bfloat16).astype(np.float64), axis, -1)
    blocks = v.reshape(v.shape[:-1] + (-1, 32))
    amax = np.abs(blocks).max(-1, keepdims=True)
    byte = np.maximum(np.where(amax > 0, np.frexp(amax)[1] - 1 + 127, 0) - down, 1)
    scale = np.exp2(byte - 127.0)
    codes = (blocks / scale).astype(np.float32).astype(dtype).astype(np.float64)
    return np.moveaxis((codes * scale).reshape(v.shape), -1, axis)


WIDE = False


def mx_kscale(k):
    if not WIDE:
        return np.ones(k)
    levels = np.array([10, -10, 5, -5, 0])
    if k % 512:
        return np.exp2(np.random.permutation(np.resize(levels, k // 32))).repeat(32)
    a = np.empty((k // 512, 16))
    for p in range(k // 512):
        a[p, :8] = np.random.permutation(np.resize(levels, 8))
        for g in range(8):
            far = levels[np.abs(levels - a[p, g]) >= 10]
            a[p, g + 8] = far[np.random.randint(len(far))]
    return np.exp2(a.ravel()).repeat(32)


def f64(x):
    return np.asarray(x).astype(np.float64)


def striped8(idx):
    return np.asarray(idx).reshape(8, -1, 16).transpose(0, 2, 1).reshape(128, -1).astype(np.uint16)


def unstriped8(offs):
    return offs.reshape(8, 16, -1).transpose(0, 2, 1).reshape(8, -1).astype(np.int64)


def pick8(x, idx, run):
    r = np.arange(len(x))
    return x[r[:, None], idx[r % (8 * run) // run]]


E2M1 = np.array([0.0, 0.5, 1.0, 1.5, 2.0, 3.0, 4.0, 6.0, -0.0, -0.5, -1.0, -1.5, -2.0, -3.0, -4.0, -6.0])


def pack_weight(w, fmt):
    k, n = w.shape
    w = f64(np.asarray(w, np.float32).astype(ml_dtypes.bfloat16)).reshape(k // 32, 32, n)
    amax = np.abs(w).max(1)
    if fmt == "e4m3":
        byte = np.frexp(amax)[1] - 1 + 127 - 7
    else:
        mant, ex = np.frexp(amax / 6.0)
        byte = np.where(mant > 0.5, ex, ex - 1) + 127
    byte = np.clip(np.where(amax > 0, byte, 1), 1, 254)
    scaled = (w * np.exp2(127.0 - byte)[:, None, :]).reshape(k, n).astype(np.float32)
    by_word = np.ascontiguousarray(scaled.reshape(k // 512, 128, 4, n).transpose(0, 1, 3, 2))
    if fmt == "e4m3":
        words = by_word.astype(ml_dtypes.float8_e4m3fn).view(np.uint8)
    else:
        c = by_word.astype(ml_dtypes.float4_e2m1fn).view(np.uint8) & 0xF
        words = (c[..., 0::2] | (c[..., 1::2] << 4)).reshape(k // 512, 128, 2 * n)
    return np.ascontiguousarray(words), np.ascontiguousarray(byte.astype(np.uint8).reshape(k // 512, 16, n))


def unpack_weight(words, scales, fmt):
    g, _, n = scales.shape
    words = np.ascontiguousarray(words).reshape(g, 128, n, -1)
    if fmt == "e4m3":
        vals = words.view(ml_dtypes.float8_e4m3fn).astype(np.float64)
    else:
        nib = np.empty((g, 128, n, 4), np.uint8)
        nib[..., 0::2] = words & 0xF
        nib[..., 1::2] = words >> 4
        vals = E2M1[nib]
    vals = vals * np.repeat(np.exp2(scales.astype(np.float64) - 127.0), 8, axis=1)[..., None]
    return vals.transpose(0, 1, 3, 2).reshape(g * 512, n)


def bf(x):
    return np.asarray(x, np.float32).astype(ml_dtypes.bfloat16)


def planes(Y):
    r, m = Y.shape
    b = f64(bf(Y)).reshape(r // 32, 32, m)
    amax = np.abs(b).max(1)
    byte = np.clip(np.where(amax > 0, np.frexp(amax)[1] - 1 + 127 - 7, 1), 1, 254)
    codes = (b * np.exp2(127.0 - byte)[:, None, :]).reshape(r, m).astype(np.float32).astype(ml_dtypes.float8_e4m3fn).view(np.uint8)
    words = codes.reshape(r // 512, 128, 4, m).transpose(0, 1, 3, 2)
    return np.ascontiguousarray(words), np.ascontiguousarray(byte.astype(np.uint8).reshape(r // 512, 16, m))


K, T, J, N = 1024, 2048, 512, 512


def setup_inputs():
    n = np.random.standard_normal
    idx = np.stack([np.random.permutation(T)[:J] for _ in range(8)])
    fk = mx_kscale(K)
    xqp = pack_weight(n((K, T)) / fk[:, None], "e2m1")
    wap = pack_weight(n((K, N)) * 1 / np.sqrt(K) * fk[:, None], "e4m3")
    wrp = pack_weight(n((K, N)) * 1 / np.sqrt(K) * fk[:, None], "e4m3")
    return {
        "xq_words": xqp[0],
        "xq_scales": xqp[1],
        "wa_words": wap[0],
        "wa_scales": wap[1],
        "rq": (n((K, J)) * 0.5 / fk[:, None]).astype(np.float32),
        "wr_words": wrp[0],
        "wr_scales": wrp[1],
        "gm": (np.random.uniform(0.5, 2.0, (N, 1))).astype(np.float32),
        "offs": striped8(idx),
    }


def reference(xq_words, xq_scales, wa_words, wa_scales, rq, wr_words, wr_scales, gm, offs):
    idx = unstriped8(offs)
    xqu = unpack_weight(xq_words, xq_scales, "e2m1")
    wau = unpack_weight(wa_words, wa_scales, "e4m3")
    wru = unpack_weight(wr_words, wr_scales, "e4m3")
    z = wau.T @ xqu
    rqq = mxq(f64(rq), 0, "e4m3")
    p = wru.T @ rqq
    pf = p * f64(gm)
    pg = np.zeros((N, T))
    pg[np.arange(N)[:, None], idx[np.arange(N) % 512 // 64]] = pf
    y = np.maximum(z + pg, 0.0)
    words, scales = planes(y)
    return y, words, scales

@@ -1,0 +1,221 @@
+from contextlib import ExitStack
+
+import concourse.mybir as mybir
+
+K, T, J, N = 1024, 2048, 512, 512
+FLOPS = 2 * K * N * (T + J)
+
+F32 = mybir.dt.float32
+BF16 = mybir.dt.bfloat16
+I32 = mybir.dt.int32
+U16 = mybir.dt.uint16
+U8 = mybir.dt.uint8
+FP8X4 = mybir.dt.float8_e4m3fn_x4
+FP4X4 = mybir.dt.float4_e2m1fn_x4
+ALU = mybir.AluOpType
+ACT = mybir.ActivationFunctionType
+
+P = 128
+PASSES = 2
+CH = 512
+NCH = T // CH
+JH = J // 2
+
+
+def tile_list_head_patches_pl_kernel(tc, xq_words, xq_scales, wa_words, wa_scales, rq, wr_words, wr_scales, gm, offs, out_0, out_1, out_2):
+    nc = tc.nc
+    with ExitStack() as ctx:
+        keep = ctx.enter_context(tc.tile_pool(name="keep", bufs=1))
+        psum = ctx.enter_context(tc.psum_pool(name="psum", bufs=1))
+
+        def sb(name, shape, dtype, tag=None):
+            return keep.tile(shape, dtype, name=name, tag=tag or name, align_bytes=64)
+
+        def bank(b, name):
+            return psum.tile([P, CH], F32, name=name, tag="bank%d" % b)
+
+        offsets = keep.tile([P, J // 16], U16, name="offsets")
+        wr_sc_raw = sb("wr_sc_raw", [P, N], U8)
+        wa_sc_raw = sb("wa_sc_raw", [P, PASSES, N], U8)
+        xq_sc = sb("xq_sc", [P, PASSES, T], U8)
+        nc.vector.memset(wr_sc_raw[:].bitcast(I32), 0)
+        nc.vector.memset(wa_sc_raw[:].bitcast(I32), 0)
+        nc.vector.memset(xq_sc[:].bitcast(I32), 0)
+        pages = {}
+        for t in (0, 1):
+            pages[t] = sb("page%d" % t, [P, T], F32)
+            nc.vector.memset(pages[t][:].bitcast(I32), 0)
+
+        rq_raw = {}
+
+        def load_rq(h, z):
+            rq_raw[h, z] = sb("rq_raw%d%d" % (h, z), [P, 4, JH], F32)
+            rows = rq[512 * z : 512 * (z + 1), :].rearrange("(p i) j -> p i j", i=4)
+            nc.sync.dma_start(out=rq_raw[h, z][:], in_=rows[:, :, JH * h : JH * (h + 1)])
+
+        def load_words(name, words):
+            raw = sb(name, [P, PASSES, N], I32)
+            nc.sync.dma_start(out=raw[:], in_=words.rearrange("z p n r -> p z (n r)").bitcast(I32))
+            return raw
+
+        load_rq(0, 0)
+        for q in range(4):
+            nc.scalar.dma_start(out=wr_sc_raw[32 * q : 32 * q + 8, :].bitcast(I32), in_=wr_scales[:, 4 * q : 4 * q + 4, :].bitcast(I32))
+        wr_raw = load_words("wr_raw", wr_words)
+        load_rq(0, 1)
+        gm_raw = sb("gm_raw", [P, 4], F32)
+        nc.sync.dma_start(out=gm_raw[:], in_=gm.rearrange("(p t) o -> p (t o)", t=4))
+        nc.sync.dma_start(offsets[:], offs)
+        wa_raw = load_words("wa_raw", wa_words)
+        for r in range(4):
+            nc.scalar.dma_start(out=wa_sc_raw[r:P:32, :, :].bitcast(I32), in_=wa_scales.rearrange("z (q r) n -> r q z n", r=4)[r].bitcast(I32))
+        load_rq(1, 0)
+        load_rq(1, 1)
+        for r in range(4):
+            nc.sync.dma_start(out=xq_sc[r:P:32, :, :].bitcast(I32), in_=xq_scales.rearrange("z (q r) c -> r q z c", r=4)[r].bitcast(I32))
+        xq = []
+        for c in range(NCH):
+            xq.append(sb("xq%d" % c, [P, PASSES, 2 * CH], U8))
+            nc.sync.dma_start(out=xq[c][:].bitcast(I32), in_=xq_words.rearrange("z p b -> p z b")[:, :, 2 * CH * c : 2 * CH * (c + 1)].bitcast(I32))
+
+        gm_t = sb("gm_t", [P, 4], F32)
+        nc.scalar.activation(gm_t[:], gm_raw[:], ACT.Copy)
+
+        def deal_words(name, raw):
+            dealt = sb(name, [P, PASSES, 4, P], I32)
+            nc.vector.tensor_copy(out=dealt[:].rearrange("p z t m -> p z m t"), in_=raw[:].rearrange("p z (m t) -> p z m t", t=4))
+            return dealt
+
+        wr = deal_words("wr", wr_raw)
+        wr_sc = sb("wr_sc", [P, 4, P], U8)
+        nc.vector.tensor_copy(out=wr_sc[:], in_=wr_sc_raw[:].rearrange("p (m t) -> p t m", t=4))
+
+        def weave_views(dst, src):
+            return dst.rearrange("p (c i) t -> p c t i", i=4), src.rearrange("p t (c i) -> p c t i", i=4)
+
+        rq_codes = {}
+        rq_sc = {}
+
+        def prep_rq(h):
+            if h == 0:
+                both = sb("rq_bf0", [P, PASSES, JH, 4], BF16, tag="page2")
+                grouped = [both[:, z] for z in range(PASSES)]
+            else:
+                grouped = [sb("rq_bf1%d" % z, [P, JH, 4], BF16, tag="rq_bf1%d" % z)[:] for z in range(PASSES)]
+            rq_codes[h] = sb("rq_codes%d" % h, [P, PASSES, JH], I32)
+            rq_sc[h] = sb("rq_sc%d" % h, [P, PASSES, JH], U8)
+            for z in range(PASSES):
+                dst, src = weave_views(grouped[z], rq_raw[h, z][:])
+                if h == 0 and z == 0:
+                    nc.vector.tensor_copy(out=dst, in_=src)
+                else:
+                    nc.scalar.activation(dst, src, ACT.Copy)
+                nc.vector.quantize_mx(out=rq_codes[h][:, z, :].bitcast(FP8X4), scales=rq_sc[h][:, z, :], in_=grouped[z].rearrange("p j i -> p (j i)"))
+
+        def p_group(acc, t, h):
+            for z in range(PASSES):
+                nc.tensor.matmul_mx(out=acc[:, JH * h : JH * (h + 1)], lhsT=wr[:, z, t, :].bitcast(FP8X4), lhsT_scale=wr_sc[4 * z : P, t, :],
+                                    rhs=rq_codes[h][:, z, :].bitcast(FP8X4), rhs_scale=rq_sc[h][:, z, :], start=(z == 0), stop=(z == PASSES - 1))
+
+        def late_page(t):
+            pages[t] = sb("page%d" % t, [P, T], F32)
+            for half in range(2):
+                nc.gpsimd.memset(pages[t][:, T // 2 * half : T // 2 * (half + 1)].bitcast(I32), 0)
+
+        def patch_half(acc, t, h, tag=None):
+            p_group(acc, t, h)
+            pf = sb("pf%d%d" % (t, h), [P, JH], F32, tag=tag)
+            nc.scalar.activation(pf[:], acc[:, JH * h : JH * (h + 1)], ACT.Copy, scale=gm_t[:, t : t + 1])
+            nc.vector.tensor_copy(pages[t][:].indirect(offsets[:, JH // 16 * h : JH // 16 * (h + 1)]), pf[:])
+
+        def patch_whole(acc, t):
+            for h in range(2):
+                p_group(acc, t, h)
+            pf = sb("pf%d" % t, [P, J], F32)
+            nc.scalar.activation(pf[:], acc[:], ACT.Copy, scale=gm_t[:, t : t + 1])
+            nc.vector.tensor_copy(pages[t][:].indirect(offsets[:]), pf[:])
+
+        prep_rq(0)
+        late_page(2)
+        wa = deal_words("wa", wa_raw)
+        wa_sc = sb("wa_sc", [P, PASSES, 4, P], U8)
+        nc.vector.tensor_copy(out=wa_sc[:], in_=wa_sc_raw[:].rearrange("p z (m t) -> p z t m", t=4))
+        p_acc = {t: bank(t, "p%d" % t) for t in (0, 1, 2)}
+        patch_half(p_acc[0], 0, 0, tag="page3")
+        late_page(3)
+        patch_half(p_acc[1], 1, 0)
+        prep_rq(1)
+        patch_half(p_acc[2], 2, 0, tag="rq_bf10")
+        for t in (0, 1, 2):
+            patch_half(p_acc[t], t, 1)
+
+        def z_group(b, t, c):
+            acc = bank(b, "z%d%d" % (t, c))
+            for z in range(PASSES):
+                nc.tensor.matmul_mx(out=acc[:], lhsT=wa[:, z, t, :].bitcast(FP8X4), lhsT_scale=wa_sc[:, z, t, :],
+                                    rhs=xq[c][:, z, :].bitcast(FP4X4), rhs_scale=xq_sc[:, z, CH * c : CH * (c + 1)], start=(z == 0), stop=(z == PASSES - 1))
+            return acc
+
+        y = {(pair, c): sb("y%d%d" % (pair, c), [P, 2, CH], F32) for pair in range(2) for c in range(NCH)}
+        rows_of = out_0.rearrange("(p t) c -> t p c", t=4)
+
+        def relu_store(s, t, c):
+            dst = y[t // 2, c][:, t % 2, :]
+            nc.scalar.activation(dst, s[:, CH * c : CH * (c + 1)], ACT.Relu)
+            nc.sync.dma_start(out=rows_of[t][:, CH * c : CH * (c + 1)], in_=dst)
+
+        z_banks = {0: (3, 4, 5, 6), 1: (7, 0, 1, 3), 2: (4, 5, 6, 7), 3: (0, 1, 2, 3)}
+        y_bf = [sb("y_bf%d" % c, [P, CH, 4], BF16) for c in range(NCH)]
+
+        def pair_views(pair, c):
+            return (y_bf[c][:, :, 2 * pair : 2 * pair + 2].rearrange("p (c i) t -> p c t i", i=4),
+                    y[pair, c][:].rearrange("p t (c i) -> p c t i", i=4))
+
+        zs = {}
+        for t in (0, 1):
+            zs[t] = sb("zs%d" % t, [P, T], F32)
+            for c in range(NCH):
+                acc = z_group(z_banks[t][c], t, c)
+                nc.scalar.copy(zs[t][:, CH * c : CH * (c + 1)], acc[:])
+        for t in (0, 1):
+            s = sb("s%d" % t, [P, T], F32, tag="s%d" % t)
+            for c in range(NCH):
+                cols = slice(CH * c, CH * (c + 1))
+                nc.gpsimd.tensor_tensor(s[:, cols], zs[t][:, cols], pages[t][:, cols], ALU.add)
+                relu_store(s, t, c)
+        for c in range(NCH):
+            dst, src = pair_views(0, c)
+            if c < 2:
+                nc.scalar.activation(dst, src, ACT.Copy)
+            else:
+                nc.gpsimd.tensor_scalar(dst, src, 1.0, 1.0, ALU.mult, ALU.mult)
+
+        s = sb("s2", [P, T], F32, tag="s0")
+        z2 = [z_group(z_banks[2][c], 2, c) for c in range(NCH)]
+        for c in range(NCH):
+            cols = slice(CH * c, CH * (c + 1))
+            nc.vector.tensor_tensor(s[:, cols], z2[c][:], pages[2][:, cols], ALU.add)
+            relu_store(s, 2, c)
+            if c == 0:
+                patch_whole(bank(z_banks[2][0], "p3"), 3)
+
+        codes = [sb("codes%d" % c, [P, CH], I32) for c in range(NCH)]
+        y_sc = sb("y_sc", [P, T], U8)
+        s = sb("s3", [P, T], F32, tag="s1")
+        z3 = [z_group(z_banks[3][c], 3, c) for c in range(NCH)]
+        words_out = out_1[0].rearrange("p c r -> p (c r)")
+        for c in range(NCH):
+            cols = slice(CH * c, CH * (c + 1))
+            nc.vector.tensor_tensor(s[:, cols], z3[c][:], pages[3][:, cols], ALU.add)
+            relu_store(s, 3, c)
+        for c in range(NCH):
+            cols = slice(CH * c, CH * (c + 1))
+            dst, src = pair_views(1, c)
+            if c >= 2:
+                nc.scalar.activation(dst, src, ACT.Copy)
+            else:
+                nc.vector.tensor_copy(out=dst, in_=src)
+            nc.vector.quantize_mx(out=codes[c][:].bitcast(FP8X4), scales=y_sc[:, cols], in_=y_bf[c][:].rearrange("p c t -> p (c t)"))
+            nc.sync.dma_start(out=words_out[:, 4 * CH * c : 4 * CH * (c + 1)].bitcast(I32), in_=codes[c][:])
+        for r in range(4):
+            nc.sync.dma_start(out=out_2[0].rearrange("(q r) c -> r q c", r=4)[r].bitcast(I32), in_=y_sc[r:P:32, :].bitcast(I32))

@@ -35,16 +35,15 @@ def tile_list_head_patches_pl_kernel(tc, xq_words, xq_scales, wa_words, wa_scale
             return psum.tile([P, CH], F32, name=name, tag="bank%d" % b)
 
         offsets = keep.tile([P, J // 16], U16, name="offsets")
-        wr_sc_raw = sb("wr_sc_raw", [P, N], U8)
-        wa_sc_raw = sb("wa_sc_raw", [P, PASSES, N], U8)
+        w_sc_raw = sb("w_sc_raw", [P, PASSES, N], U8)
         xq_sc = sb("xq_sc", [P, PASSES, T], U8)
-        nc.vector.memset(wr_sc_raw[:].bitcast(I32), 0)
-        nc.vector.memset(wa_sc_raw[:].bitcast(I32), 0)
+        nc.vector.memset(w_sc_raw[:].bitcast(I32), 0)
         nc.vector.memset(xq_sc[:].bitcast(I32), 0)
-        pages = {}
-        for t in (0, 1):
-            pages[t] = sb("page%d" % t, [P, T], F32)
-            nc.vector.memset(pages[t][:].bitcast(I32), 0)
+        page_a = sb("page_a", [P, T], F32)
+        nc.vector.memset(page_a[:], 0.0)
+        page_b = sb("page_b", [P, T], F32)
+        nc.vector.memset(page_b[:], 0.0)
+        pages = {0: page_a, 1: page_b, 2: page_b, 3: page_b}
 
         rq_raw = {}
 
@@ -59,16 +58,15 @@ def tile_list_head_patches_pl_kernel(tc, xq_words, xq_scales, wa_words, wa_scale
             return raw
 
         load_rq(0, 0)
-        for q in range(4):
-            nc.scalar.dma_start(out=wr_sc_raw[32 * q : 32 * q + 8, :].bitcast(I32), in_=wr_scales[:, 4 * q : 4 * q + 4, :].bitcast(I32))
+        for first, scales in ((4, wr_scales), (0, wa_scales)):
+            for r in range(4):
+                nc.scalar.dma_start(out=w_sc_raw[first + r : P : 32, :, :].bitcast(I32), in_=scales.rearrange("z (q r) n -> r q z n", r=4)[r].bitcast(I32))
         wr_raw = load_words("wr_raw", wr_words)
         load_rq(0, 1)
         gm_raw = sb("gm_raw", [P, 4], F32)
         nc.sync.dma_start(out=gm_raw[:], in_=gm.rearrange("(p t) o -> p (t o)", t=4))
         nc.sync.dma_start(offsets[:], offs)
         wa_raw = load_words("wa_raw", wa_words)
-        for r in range(4):
-            nc.scalar.dma_start(out=wa_sc_raw[r:P:32, :, :].bitcast(I32), in_=wa_scales.rearrange("z (q r) n -> r q z n", r=4)[r].bitcast(I32))
         load_rq(1, 0)
         load_rq(1, 1)
         for r in range(4):
@@ -87,8 +85,8 @@ def tile_list_head_patches_pl_kernel(tc, xq_words, xq_scales, wa_words, wa_scale
             return dealt
 
         wr = deal_words("wr", wr_raw)
-        wr_sc = sb("wr_sc", [P, 4, P], U8)
-        nc.vector.tensor_copy(out=wr_sc[:], in_=wr_sc_raw[:].rearrange("p (m t) -> p t m", t=4))
+        w_sc = sb("w_sc", [P, PASSES, 4, P], U8)
+        nc.vector.tensor_copy(out=w_sc[:], in_=w_sc_raw[:].rearrange("p z (m t) -> p z t m", t=4))
 
         def weave_views(dst, src):
             return dst.rearrange("p (c i) t -> p c t i", i=4), src.rearrange("p t (c i) -> p c t i", i=4)
@@ -97,62 +95,49 @@ def tile_list_head_patches_pl_kernel(tc, xq_words, xq_scales, wa_words, wa_scale
         rq_sc = {}
 
         def prep_rq(h):
-            if h == 0:
-                both = sb("rq_bf0", [P, PASSES, JH, 4], BF16, tag="page2")
-                grouped = [both[:, z] for z in range(PASSES)]
-            else:
-                grouped = [sb("rq_bf1%d" % z, [P, JH, 4], BF16, tag="rq_bf1%d" % z)[:] for z in range(PASSES)]
+            grouped = sb("rq_bf%d" % h, [P, PASSES, JH, 4], BF16, tag="late_page%d" % h)
             rq_codes[h] = sb("rq_codes%d" % h, [P, PASSES, JH], I32)
             rq_sc[h] = sb("rq_sc%d" % h, [P, PASSES, JH], U8)
             for z in range(PASSES):
-                dst, src = weave_views(grouped[z], rq_raw[h, z][:])
-                if h == 0 and z == 0:
-                    nc.vector.tensor_copy(out=dst, in_=src)
-                else:
-                    nc.scalar.activation(dst, src, ACT.Copy)
-                nc.vector.quantize_mx(out=rq_codes[h][:, z, :].bitcast(FP8X4), scales=rq_sc[h][:, z, :], in_=grouped[z].rearrange("p j i -> p (j i)"))
+                dst, src = weave_views(grouped[:, z], rq_raw[h, z][:])
+                nc.scalar.activation(dst, src, ACT.Copy)
+                nc.vector.quantize_mx(out=rq_codes[h][:, z, :].bitcast(FP8X4), scales=rq_sc[h][:, z, :], in_=grouped[:, z].rearrange("p j i -> p (j i)"))
 
         def p_group(acc, t, h):
             for z in range(PASSES):
-                nc.tensor.matmul_mx(out=acc[:, JH * h : JH * (h + 1)], lhsT=wr[:, z, t, :].bitcast(FP8X4), lhsT_scale=wr_sc[4 * z : P, t, :],
+                nc.tensor.matmul_mx(out=acc[:, JH * h : JH * (h + 1)], lhsT=wr[:, z, t, :].bitcast(FP8X4), lhsT_scale=w_sc[4:P, z, t, :],
                                     rhs=rq_codes[h][:, z, :].bitcast(FP8X4), rhs_scale=rq_sc[h][:, z, :], start=(z == 0), stop=(z == PASSES - 1))
 
-        def late_page(t):
-            pages[t] = sb("page%d" % t, [P, T], F32)
-            for half in range(2):
-                nc.gpsimd.memset(pages[t][:, T // 2 * half : T // 2 * (half + 1)].bitcast(I32), 0)
-
-        def patch_half(acc, t, h, tag=None):
+        def patch_half(acc, t, h):
             p_group(acc, t, h)
-            pf = sb("pf%d%d" % (t, h), [P, JH], F32, tag=tag)
+            pf = sb("pf%d%d" % (t, h), [P, JH], F32)
             nc.scalar.activation(pf[:], acc[:, JH * h : JH * (h + 1)], ACT.Copy, scale=gm_t[:, t : t + 1])
             nc.vector.tensor_copy(pages[t][:].indirect(offsets[:, JH // 16 * h : JH // 16 * (h + 1)]), pf[:])
 
-        def patch_whole(acc, t):
+        def make_pf(acc, t):
             for h in range(2):
                 p_group(acc, t, h)
             pf = sb("pf%d" % t, [P, J], F32)
             nc.scalar.activation(pf[:], acc[:], ACT.Copy, scale=gm_t[:, t : t + 1])
+            return pf
+
+        def scatter_whole(pf, t):
             nc.vector.tensor_copy(pages[t][:].indirect(offsets[:]), pf[:])
 
         prep_rq(0)
-        late_page(2)
         wa = deal_words("wa", wa_raw)
-        wa_sc = sb("wa_sc", [P, PASSES, 4, P], U8)
-        nc.vector.tensor_copy(out=wa_sc[:], in_=wa_sc_raw[:].rearrange("p z (m t) -> p z t m", t=4))
-        p_acc = {t: bank(t, "p%d" % t) for t in (0, 1, 2)}
-        patch_half(p_acc[0], 0, 0, tag="page3")
-        late_page(3)
-        patch_half(p_acc[1], 1, 0)
+        p_acc = {t: bank(t, "p%d" % t) for t in (0, 1)}
+        for t in (0, 1):
+            patch_half(p_acc[t], t, 0)
         prep_rq(1)
-        patch_half(p_acc[2], 2, 0, tag="rq_bf10")
-        for t in (0, 1, 2):
+        for t in (0, 1):
             patch_half(p_acc[t], t, 1)
+        pf_late = {t: make_pf(bank(t, "p%d" % t), t) for t in (2, 3)}
 
         def z_group(b, t, c):
             acc = bank(b, "z%d%d" % (t, c))
             for z in range(PASSES):
-                nc.tensor.matmul_mx(out=acc[:], lhsT=wa[:, z, t, :].bitcast(FP8X4), lhsT_scale=wa_sc[:, z, t, :],
+                nc.tensor.matmul_mx(out=acc[:], lhsT=wa[:, z, t, :].bitcast(FP8X4), lhsT_scale=w_sc[:, z, t, :],
                                     rhs=xq[c][:, z, :].bitcast(FP4X4), rhs_scale=xq_sc[:, z, CH * c : CH * (c + 1)], start=(z == 0), stop=(z == PASSES - 1))
             return acc
 
@@ -164,50 +149,28 @@ def tile_list_head_patches_pl_kernel(tc, xq_words, xq_scales, wa_words, wa_scale
             nc.scalar.activation(dst, s[:, CH * c : CH * (c + 1)], ACT.Relu)
             nc.sync.dma_start(out=rows_of[t][:, CH * c : CH * (c + 1)], in_=dst)
 
-        z_banks = {0: (3, 4, 5, 6), 1: (7, 0, 1, 3), 2: (4, 5, 6, 7), 3: (0, 1, 2, 3)}
         y_bf = [sb("y_bf%d" % c, [P, CH, 4], BF16) for c in range(NCH)]
 
         def pair_views(pair, c):
-            return (y_bf[c][:, :, 2 * pair : 2 * pair + 2].rearrange("p (c i) t -> p c t i", i=4),
-                    y[pair, c][:].rearrange("p t (c i) -> p c t i", i=4))
+            return y_bf[c][:, :, 2 * pair : 2 * pair + 2], y[pair, c][:].rearrange("p t c -> p c t")
 
-        zs = {}
-        for t in (0, 1):
-            zs[t] = sb("zs%d" % t, [P, T], F32)
-            for c in range(NCH):
-                acc = z_group(z_banks[t][c], t, c)
-                nc.scalar.copy(zs[t][:, CH * c : CH * (c + 1)], acc[:])
-        for t in (0, 1):
-            s = sb("s%d" % t, [P, T], F32, tag="s%d" % t)
+        for t in range(4):
+            if t >= 2:
+                scatter_whole(pf_late[t], t)
+            s = sb("s%d" % t, [P, T], F32)
             for c in range(NCH):
                 cols = slice(CH * c, CH * (c + 1))
-                nc.gpsimd.tensor_tensor(s[:, cols], zs[t][:, cols], pages[t][:, cols], ALU.add)
+                acc = z_group((4 if t % 2 == 0 else 0) + c, t, c)
+                nc.vector.tensor_tensor(s[:, cols], acc[:], pages[t][:, cols], ALU.add)
                 relu_store(s, t, c)
-        for c in range(NCH):
-            dst, src = pair_views(0, c)
-            if c < 2:
-                nc.scalar.activation(dst, src, ACT.Copy)
-            else:
-                nc.gpsimd.tensor_scalar(dst, src, 1.0, 1.0, ALU.mult, ALU.mult)
-
-        s = sb("s2", [P, T], F32, tag="s0")
-        z2 = [z_group(z_banks[2][c], 2, c) for c in range(NCH)]
-        for c in range(NCH):
-            cols = slice(CH * c, CH * (c + 1))
-            nc.vector.tensor_tensor(s[:, cols], z2[c][:], pages[2][:, cols], ALU.add)
-            relu_store(s, 2, c)
-            if c == 0:
-                patch_whole(bank(z_banks[2][0], "p3"), 3)
+            if t == 1:
+                for c in range(NCH):
+                    dst, src = pair_views(0, c)
+                    nc.scalar.activation(dst, src, ACT.Copy)
 
         codes = [sb("codes%d" % c, [P, CH], I32) for c in range(NCH)]
         y_sc = sb("y_sc", [P, T], U8)
-        s = sb("s3", [P, T], F32, tag="s1")
-        z3 = [z_group(z_banks[3][c], 3, c) for c in range(NCH)]
         words_out = out_1[0].rearrange("p c r -> p (c r)")
-        for c in range(NCH):
-            cols = slice(CH * c, CH * (c + 1))
-            nc.vector.tensor_tensor(s[:, cols], z3[c][:], pages[3][:, cols], ALU.add)
-            relu_store(s, 3, c)
         for c in range(NCH):
             cols = slice(CH * c, CH * (c + 1))
             dst, src = pair_views(1, c)

@@ -35,15 +35,17 @@ def tile_list_head_patches_pl_kernel(tc, xq_words, xq_scales, wa_words, wa_scale
             return psum.tile([P, CH], F32, name=name, tag="bank%d" % b)
 
         offsets = keep.tile([P, J // 16], U16, name="offsets")
-        w_sc_raw = sb("w_sc_raw", [P, PASSES, N], U8)
+        wr_sc_raw = sb("wr_sc_raw", [P, N], U8)
+        wa_sc_raw = sb("wa_sc_raw", [P, PASSES, N], U8)
         xq_sc = sb("xq_sc", [P, PASSES, T], U8)
-        nc.vector.memset(w_sc_raw[:].bitcast(I32), 0)
-        nc.vector.memset(xq_sc[:].bitcast(I32), 0)
+        nc.vector.memset(wr_sc_raw[:].bitcast(I32), 0)
+        nc.vector.memset(wa_sc_raw[:].bitcast(I32), 0)
         page_a = sb("page_a", [P, T], F32)
-        nc.vector.memset(page_a[:], 0.0)
         page_b = sb("page_b", [P, T], F32)
-        nc.vector.memset(page_b[:], 0.0)
-        pages = {0: page_a, 1: page_b, 2: page_b, 3: page_b}
+        nc.vector.memset(page_a[:].bitcast(I32), 0)
+        nc.vector.memset(page_b[:].bitcast(I32), 0)
+        nc.vector.memset(xq_sc[:].bitcast(I32), 0)
+        pages = (page_a, page_b, page_b, page_a)
 
         rq_raw = {}
 
@@ -58,17 +60,18 @@ def tile_list_head_patches_pl_kernel(tc, xq_words, xq_scales, wa_words, wa_scale
             return raw
 
         load_rq(0, 0)
-        for first, scales in ((4, wr_scales), (0, wa_scales)):
-            for r in range(4):
-                nc.scalar.dma_start(out=w_sc_raw[first + r : P : 32, :, :].bitcast(I32), in_=scales.rearrange("z (q r) n -> r q z n", r=4)[r].bitcast(I32))
-        wr_raw = load_words("wr_raw", wr_words)
+        for q in range(4):
+            nc.scalar.dma_start(out=wr_sc_raw[32 * q : 32 * q + 8, :].bitcast(I32), in_=wr_scales[:, 4 * q : 4 * q + 4, :].bitcast(I32))
         load_rq(0, 1)
+        wr_raw = load_words("wr_raw", wr_words)
         gm_raw = sb("gm_raw", [P, 4], F32)
         nc.sync.dma_start(out=gm_raw[:], in_=gm.rearrange("(p t) o -> p (t o)", t=4))
-        nc.sync.dma_start(offsets[:], offs)
-        wa_raw = load_words("wa_raw", wa_words)
         load_rq(1, 0)
         load_rq(1, 1)
+        nc.sync.dma_start(offsets[:], offs)
+        for r in range(4):
+            nc.gpsimd.dma_start(out=wa_sc_raw[r:P:32, :, :].bitcast(I32), in_=wa_scales.rearrange("z (q r) n -> r q z n", r=4)[r].bitcast(I32))
+        wa_raw = load_words("wa_raw", wa_words)
         for r in range(4):
             nc.sync.dma_start(out=xq_sc[r:P:32, :, :].bitcast(I32), in_=xq_scales.rearrange("z (q r) c -> r q z c", r=4)[r].bitcast(I32))
         xq = []
@@ -76,17 +79,16 @@ def tile_list_head_patches_pl_kernel(tc, xq_words, xq_scales, wa_words, wa_scale
             xq.append(sb("xq%d" % c, [P, PASSES, 2 * CH], U8))
             nc.sync.dma_start(out=xq[c][:].bitcast(I32), in_=xq_words.rearrange("z p b -> p z b")[:, :, 2 * CH * c : 2 * CH * (c + 1)].bitcast(I32))
 
-        gm_t = sb("gm_t", [P, 4], F32)
+        gm_t = sb("gm_t", [P, 4], F32, tag="late_page1")
         nc.scalar.activation(gm_t[:], gm_raw[:], ACT.Copy)
 
-        def deal_words(name, raw):
-            dealt = sb(name, [P, PASSES, 4, P], I32)
+        def deal_words(name, raw, tag=None):
+            dealt = sb(name, [P, PASSES, 4, P], I32, tag=tag)
             nc.vector.tensor_copy(out=dealt[:].rearrange("p z t m -> p z m t"), in_=raw[:].rearrange("p z (m t) -> p z m t", t=4))
             return dealt
 
-        wr = deal_words("wr", wr_raw)
-        w_sc = sb("w_sc", [P, PASSES, 4, P], U8)
-        nc.vector.tensor_copy(out=w_sc[:], in_=w_sc_raw[:].rearrange("p z (m t) -> p z t m", t=4))
+        wr_sc = sb("wr_sc", [P, 4, P], U8)
+        nc.vector.tensor_copy(out=wr_sc[:], in_=wr_sc_raw[:].rearrange("p (m t) -> p t m", t=4))
 
         def weave_views(dst, src):
             return dst.rearrange("p (c i) t -> p c t i", i=4), src.rearrange("p t (c i) -> p c t i", i=4)
@@ -99,37 +101,49 @@ def tile_list_head_patches_pl_kernel(tc, xq_words, xq_scales, wa_words, wa_scale
             rq_codes[h] = sb("rq_codes%d" % h, [P, PASSES, JH], I32)
             rq_sc[h] = sb("rq_sc%d" % h, [P, PASSES, JH], U8)
             for z in range(PASSES):
-                dst, src = weave_views(grouped[:, z], rq_raw[h, z][:])
+                if h == 0 and z == 1:
+                    cut = 192
+                    dst, src = weave_views(grouped[:, z, :cut], rq_raw[h, z][:, :, :cut])
+                    nc.vector.tensor_copy(out=dst, in_=src)
+                    dst, src = weave_views(grouped[:, z, cut:], rq_raw[h, z][:, :, cut:])
+                else:
+                    dst, src = weave_views(grouped[:, z], rq_raw[h, z][:])
                 nc.scalar.activation(dst, src, ACT.Copy)
                 nc.vector.quantize_mx(out=rq_codes[h][:, z, :].bitcast(FP8X4), scales=rq_sc[h][:, z, :], in_=grouped[:, z].rearrange("p j i -> p (j i)"))
 
         def p_group(acc, t, h):
             for z in range(PASSES):
-                nc.tensor.matmul_mx(out=acc[:, JH * h : JH * (h + 1)], lhsT=wr[:, z, t, :].bitcast(FP8X4), lhsT_scale=w_sc[4:P, z, t, :],
+                nc.tensor.matmul_mx(out=acc[:, JH * h : JH * (h + 1)], lhsT=wr_half[t // 2][:, z, t % 2, :].bitcast(FP8X4), lhsT_scale=wr_sc[4 * z : P, t, :],
                                     rhs=rq_codes[h][:, z, :].bitcast(FP8X4), rhs_scale=rq_sc[h][:, z, :], start=(z == 0), stop=(z == PASSES - 1))
 
         def patch_half(acc, t, h):
             p_group(acc, t, h)
             pf = sb("pf%d%d" % (t, h), [P, JH], F32)
-            nc.scalar.activation(pf[:], acc[:, JH * h : JH * (h + 1)], ACT.Copy, scale=gm_t[:, t : t + 1])
+            nc.scalar.activation(pf[:], acc[:, JH * h : JH * (h + 1)], ACT.Copy, scale=(gm_t if h == 0 else gm_raw)[:, t : t + 1])
             nc.vector.tensor_copy(pages[t][:].indirect(offsets[:, JH // 16 * h : JH // 16 * (h + 1)]), pf[:])
 
         def make_pf(acc, t):
             for h in range(2):
                 p_group(acc, t, h)
             pf = sb("pf%d" % t, [P, J], F32)
-            nc.scalar.activation(pf[:], acc[:], ACT.Copy, scale=gm_t[:, t : t + 1])
+            nc.scalar.activation(pf[:], acc[:], ACT.Copy, scale=gm_raw[:, t : t + 1])
             return pf
 
         def scatter_whole(pf, t):
             nc.vector.tensor_copy(pages[t][:].indirect(offsets[:]), pf[:])
 
         prep_rq(0)
-        wa = deal_words("wa", wa_raw)
+        wr_half = []
+        for u in range(2):
+            wr_half.append(sb("wr%d" % u, [P, PASSES, 2, P], I32))
+            nc.vector.tensor_copy(out=wr_half[u][:].rearrange("p z t m -> p z m t"), in_=wr_raw[:].rearrange("p z (m t) -> p z m t", t=4)[:, :, :, 2 * u : 2 * u + 2])
         p_acc = {t: bank(t, "p%d" % t) for t in (0, 1)}
         for t in (0, 1):
             patch_half(p_acc[t], t, 0)
         prep_rq(1)
+        wa = deal_words("wa", wa_raw, tag="late_page1")
+        wa_sc = sb("wa_sc", [P, PASSES, 4, P], U8, tag="rq_raw11")
+        nc.vector.tensor_copy(out=wa_sc[:], in_=wa_sc_raw[:].rearrange("p z (m t) -> p z t m", t=4))
         for t in (0, 1):
             patch_half(p_acc[t], t, 1)
         pf_late = {t: make_pf(bank(t, "p%d" % t), t) for t in (2, 3)}
@@ -137,48 +151,75 @@ def tile_list_head_patches_pl_kernel(tc, xq_words, xq_scales, wa_words, wa_scale
         def z_group(b, t, c):
             acc = bank(b, "z%d%d" % (t, c))
             for z in range(PASSES):
-                nc.tensor.matmul_mx(out=acc[:], lhsT=wa[:, z, t, :].bitcast(FP8X4), lhsT_scale=w_sc[:, z, t, :],
+                nc.tensor.matmul_mx(out=acc[:], lhsT=wa[:, z, t, :].bitcast(FP8X4), lhsT_scale=wa_sc[:, z, t, :],
                                     rhs=xq[c][:, z, :].bitcast(FP4X4), rhs_scale=xq_sc[:, z, CH * c : CH * (c + 1)], start=(z == 0), stop=(z == PASSES - 1))
             return acc
 
-        y = {(pair, c): sb("y%d%d" % (pair, c), [P, 2, CH], F32) for pair in range(2) for c in range(NCH)}
         rows_of = out_0.rearrange("(p t) c -> t p c", t=4)
 
-        def relu_store(s, t, c):
-            dst = y[t // 2, c][:, t % 2, :]
-            nc.scalar.activation(dst, s[:, CH * c : CH * (c + 1)], ACT.Relu)
-            nc.sync.dma_start(out=rows_of[t][:, CH * c : CH * (c + 1)], in_=dst)
-
+        s = {(pair, c): sb("s%d%d" % (pair, c), [P, 2, CH], F32) for pair in range(2) for c in range(NCH)}
         y_bf = [sb("y_bf%d" % c, [P, CH, 4], BF16) for c in range(NCH)]
-
-        def pair_views(pair, c):
-            return y_bf[c][:, :, 2 * pair : 2 * pair + 2], y[pair, c][:].rearrange("p t c -> p c t")
-
-        for t in range(4):
-            if t >= 2:
-                scatter_whole(pf_late[t], t)
-            s = sb("s%d" % t, [P, T], F32)
-            for c in range(NCH):
-                cols = slice(CH * c, CH * (c + 1))
-                acc = z_group((4 if t % 2 == 0 else 0) + c, t, c)
-                nc.vector.tensor_tensor(s[:, cols], acc[:], pages[t][:, cols], ALU.add)
-                relu_store(s, t, c)
-            if t == 1:
-                for c in range(NCH):
-                    dst, src = pair_views(0, c)
-                    nc.scalar.activation(dst, src, ACT.Copy)
-
-        codes = [sb("codes%d" % c, [P, CH], I32) for c in range(NCH)]
         y_sc = sb("y_sc", [P, T], U8)
         words_out = out_1[0].rearrange("p c r -> p (c r)")
-        for c in range(NCH):
-            cols = slice(CH * c, CH * (c + 1))
-            dst, src = pair_views(1, c)
-            if c >= 2:
-                nc.scalar.activation(dst, src, ACT.Copy)
+        z_banks = ((4, 5, 6, 7), (0, 1, 2, 3), (4, 0, 1, 2), (3, 5, 6, 7))
+
+        def add(t, c):
+            acc = z_group(z_banks[t][c], t, c)
+            nc.vector.tensor_tensor(s[t // 2, c][:, t % 2, :], acc[:], pages[t][:, CH * c : CH * (c + 1)], ALU.add)
+
+        def relu(t, c):
+            y = sb("y%d%d" % (t, c), [P, CH], F32)
+            nc.scalar.activation(y[:], s[t // 2, c][:, t % 2, :], ACT.Relu)
+            nc.sync.dma_start(out=rows_of[t][:, CH * c : CH * (c + 1)], in_=y[:])
+
+        def weave(pair, c, on_scalar):
+            dst, src = y_bf[c][:, :, 2 * pair : 2 * pair + 2], s[pair, c][:].rearrange("p t c -> p c t")
+            if on_scalar:
+                nc.scalar.activation(dst, src, ACT.Relu)
             else:
-                nc.vector.tensor_copy(out=dst, in_=src)
-            nc.vector.quantize_mx(out=codes[c][:].bitcast(FP8X4), scales=y_sc[:, cols], in_=y_bf[c][:].rearrange("p c t -> p (c t)"))
-            nc.sync.dma_start(out=words_out[:, 4 * CH * c : 4 * CH * (c + 1)].bitcast(I32), in_=codes[c][:])
+                nc.vector.tensor_scalar_max(dst, src, 0.0)
+
+        def planes(c):
+            nc.vector.quantize_mx(out=codes[:, CH * c : CH * (c + 1)].bitcast(FP8X4), scales=y_sc[:, CH * c : CH * (c + 1)], in_=y_bf[c][:].rearrange("p c t -> p (c t)"))
+            nc.sync.dma_start(out=words_out[:, 4 * CH * c : 4 * CH * (c + 1)].bitcast(I32), in_=codes[:, CH * c : CH * (c + 1)])
+
+        def both(t, c):
+            add(t, c)
+            relu(t, c)
+
+        both(0, 0)
+        both(1, 0)
+        weave(0, 0, True)
+        for c in (1, 2, 3):
+            both(1, c)
+        both(0, 1)
+        weave(0, 1, True)
+        scatter_whole(pf_late[2], 2)
+        both(0, 2)
+        weave(0, 2, True)
+        both(2, 0)
+        both(2, 1)
+        both(0, 3)
+        weave(0, 3, True)
+        both(2, 2)
+        codes = sb("codes", [P, T], I32, tag="y22")
+        scatter_whole(pf_late[3], 3)
+        both(2, 3)
+        add(3, 0)
+        weave(1, 0, True)
+        relu(3, 0)
+        both(3, 1)
+        add(3, 2)
+        add(3, 3)
+        weave(1, 1, False)
+        planes(0)
+        relu(3, 2)
+        weave(1, 3, True)
+        planes(1)
+        weave(1, 2, False)
+        relu(3, 3)
+        planes(2)
+        planes(3)
         for r in range(4):
-            nc.sync.dma_start(out=out_2[0].rearrange("(q r) c -> r q c", r=4)[r].bitcast(I32), in_=y_sc[r:P:32, :].bitcast(I32))
+            queue = nc.scalar if r % 2 == 0 else nc.sync
+            queue.dma_start(out=out_2[0].rearrange("(q r) c -> r q c", r=4)[r].bitcast(I32), in_=y_sc[r:P:32, :].bitcast(I32))

@@ -37,14 +37,12 @@ def tile_list_head_patches_pl_kernel(tc, xq_words, xq_scales, wa_words, wa_scale
         offsets = keep.tile([P, J // 16], U16, name="offsets")
         wr_sc_raw = sb("wr_sc_raw", [P, N], U8)
         wa_sc_raw = sb("wa_sc_raw", [P, PASSES, N], U8)
-        xq_sc = sb("xq_sc", [P, PASSES, T], U8)
         nc.vector.memset(wr_sc_raw[:].bitcast(I32), 0)
         nc.vector.memset(wa_sc_raw[:].bitcast(I32), 0)
         page_a = sb("page_a", [P, T], F32)
         page_b = sb("page_b", [P, T], F32)
         nc.vector.memset(page_a[:].bitcast(I32), 0)
         nc.vector.memset(page_b[:].bitcast(I32), 0)
-        nc.vector.memset(xq_sc[:].bitcast(I32), 0)
         pages = (page_a, page_b, page_b, page_a)
 
         rq_raw = {}
@@ -66,14 +64,12 @@ def tile_list_head_patches_pl_kernel(tc, xq_words, xq_scales, wa_words, wa_scale
         wr_raw = load_words("wr_raw", wr_words)
         gm_raw = sb("gm_raw", [P, 4], F32)
         nc.sync.dma_start(out=gm_raw[:], in_=gm.rearrange("(p t) o -> p (t o)", t=4))
+        nc.sync.dma_start(offsets[:], offs)
         load_rq(1, 0)
         load_rq(1, 1)
-        nc.sync.dma_start(offsets[:], offs)
         for r in range(4):
             nc.gpsimd.dma_start(out=wa_sc_raw[r:P:32, :, :].bitcast(I32), in_=wa_scales.rearrange("z (q r) n -> r q z n", r=4)[r].bitcast(I32))
         wa_raw = load_words("wa_raw", wa_words)
-        for r in range(4):
-            nc.sync.dma_start(out=xq_sc[r:P:32, :, :].bitcast(I32), in_=xq_scales.rearrange("z (q r) c -> r q z c", r=4)[r].bitcast(I32))
         xq = []
         for c in range(NCH):
             xq.append(sb("xq%d" % c, [P, PASSES, 2 * CH], U8))
@@ -91,7 +87,7 @@ def tile_list_head_patches_pl_kernel(tc, xq_words, xq_scales, wa_words, wa_scale
         nc.vector.tensor_copy(out=wr_sc[:], in_=wr_sc_raw[:].rearrange("p (m t) -> p t m", t=4))
 
         def weave_views(dst, src):
-            return dst.rearrange("p (c i) t -> p c t i", i=4), src.rearrange("p t (c i) -> p c t i", i=4)
+            return dst.rearrange("p (c i) t -> p c t i", i=2), src.rearrange("p t (c i) -> p c t i", i=2)
 
         rq_codes = {}
         rq_sc = {}
@@ -137,6 +133,10 @@ def tile_list_head_patches_pl_kernel(tc, xq_words, xq_scales, wa_words, wa_scale
         for u in range(2):
             wr_half.append(sb("wr%d" % u, [P, PASSES, 2, P], I32))
             nc.vector.tensor_copy(out=wr_half[u][:].rearrange("p z t m -> p z m t"), in_=wr_raw[:].rearrange("p z (m t) -> p z m t", t=4)[:, :, :, 2 * u : 2 * u + 2])
+        xq_sc = sb("xq_sc", [P, PASSES, T], U8, tag="wr_raw")
+        nc.vector.memset(xq_sc[:].bitcast(I32), 0)
+        for r in range(4):
+            nc.sync.dma_start(out=xq_sc[r:P:32, :, :].bitcast(I32), in_=xq_scales.rearrange("z (q r) c -> r q z c", r=4)[r].bitcast(I32))
         p_acc = {t: bank(t, "p%d" % t) for t in (0, 1)}
         for t in (0, 1):
             patch_half(p_acc[t], t, 0)
@@ -172,8 +172,13 @@ def tile_list_head_patches_pl_kernel(tc, xq_words, xq_scales, wa_words, wa_scale
             nc.scalar.activation(y[:], s[t // 2, c][:, t % 2, :], ACT.Relu)
             nc.sync.dma_start(out=rows_of[t][:, CH * c : CH * (c + 1)], in_=y[:])
 
-        def weave(pair, c, on_scalar):
-            dst, src = y_bf[c][:, :, 2 * pair : 2 * pair + 2], s[pair, c][:].rearrange("p t c -> p c t")
+        pairs = [sb("pairs%d" % c, [P, 2, CH, 2], BF16) for c in range(NCH)]
+
+        def merge(c):
+            nc.vector.tensor_copy(out=y_bf[c][:].bitcast(I32), in_=pairs[c][:].rearrange("p u c t -> p u (c t)").bitcast(I32).rearrange("p u c -> p c u"))
+
+        def weave(pair, c, on_scalar, lo=0, hi=CH):
+            dst, src = pairs[c][:, pair, lo:hi, :], s[pair, c][:, :, lo:hi].rearrange("p t c -> p c t")
             if on_scalar:
                 nc.scalar.activation(dst, src, ACT.Relu)
             else:
@@ -205,20 +210,24 @@ def tile_list_head_patches_pl_kernel(tc, xq_words, xq_scales, wa_words, wa_scale
         codes = sb("codes", [P, T], I32, tag="y22")
         scatter_whole(pf_late[3], 3)
         both(2, 3)
-        add(3, 0)
+        for c in range(NCH):
+            add(3, c)
         weave(1, 0, True)
+        weave(1, 1, True)
+        weave(1, 3, False, CH // 2, CH)
         relu(3, 0)
-        both(3, 1)
-        add(3, 2)
-        add(3, 3)
-        weave(1, 1, False)
+        weave(1, 2, True)
+        weave(1, 3, True, 0, CH // 2)
+        merge(0)
+        merge(1)
         planes(0)
-        relu(3, 2)
-        weave(1, 3, True)
+        relu(3, 1)
+        merge(2)
         planes(1)
-        weave(1, 2, False)
-        relu(3, 3)
+        relu(3, 2)
+        merge(3)
         planes(2)
+        relu(3, 3)
         planes(3)
         for r in range(4):
             queue = nc.scalar if r % 2 == 0 else nc.sync

@@ -20,6 +20,9 @@ PASSES = 2
 CH = 512
 NCH = T // CH
 JH = J // 2
+RQ_ON_VECTOR = 192
+F32_MAX = 3.4028234663852886e38
+SCALAR, VECTOR, GPSIMD = "scalar", "vector", "gpsimd"
 
 
 def tile_list_head_patches_pl_kernel(tc, xq_words, xq_scales, wa_words, wa_scales, rq, wr_words, wr_scales, gm, offs, out_0, out_1, out_2):
@@ -57,177 +60,197 @@ def tile_list_head_patches_pl_kernel(tc, xq_words, xq_scales, wa_words, wa_scale
             nc.sync.dma_start(out=raw[:], in_=words.rearrange("z p n r -> p z (n r)").bitcast(I32))
             return raw
 
+        def load_plane(queue, plane, scales):
+            for r in range(4):
+                queue.dma_start(out=plane[r:P:32, :, :].bitcast(I32), in_=scales.rearrange("z (q r) c -> r q z c", r=4)[r].bitcast(I32))
+
         load_rq(0, 0)
         for q in range(4):
             nc.scalar.dma_start(out=wr_sc_raw[32 * q : 32 * q + 8, :].bitcast(I32), in_=wr_scales[:, 4 * q : 4 * q + 4, :].bitcast(I32))
         load_rq(0, 1)
         wr_raw = load_words("wr_raw", wr_words)
-        gm_raw = sb("gm_raw", [P, 4], F32)
-        nc.sync.dma_start(out=gm_raw[:], in_=gm.rearrange("(p t) o -> p (t o)", t=4))
+        gm_dealt = sb("gm_dealt", [P, 4], F32)
+        nc.sync.dma_start(out=gm_dealt[:], in_=gm.rearrange("(p t) o -> p (t o)", t=4))
         nc.sync.dma_start(offsets[:], offs)
         load_rq(1, 0)
         load_rq(1, 1)
-        for r in range(4):
-            nc.gpsimd.dma_start(out=wa_sc_raw[r:P:32, :, :].bitcast(I32), in_=wa_scales.rearrange("z (q r) n -> r q z n", r=4)[r].bitcast(I32))
+        load_plane(nc.gpsimd, wa_sc_raw, wa_scales)
         wa_raw = load_words("wa_raw", wa_words)
         xq = []
         for c in range(NCH):
             xq.append(sb("xq%d" % c, [P, PASSES, 2 * CH], U8))
             nc.sync.dma_start(out=xq[c][:].bitcast(I32), in_=xq_words.rearrange("z p b -> p z b")[:, :, 2 * CH * c : 2 * CH * (c + 1)].bitcast(I32))
 
-        gm_t = sb("gm_t", [P, 4], F32, tag="late_page1")
-        nc.scalar.activation(gm_t[:], gm_raw[:], ACT.Copy)
-
-        def deal_words(name, raw, tag=None):
-            dealt = sb(name, [P, PASSES, 4, P], I32, tag=tag)
-            nc.vector.tensor_copy(out=dealt[:].rearrange("p z t m -> p z m t"), in_=raw[:].rearrange("p z (m t) -> p z m t", t=4))
-            return dealt
+        gm_first = sb("gm_first", [P, 4], F32, tag="rq_bf1")
+        nc.scalar.activation(gm_first[:], gm_dealt[:], ACT.Copy)
 
         wr_sc = sb("wr_sc", [P, 4, P], U8)
         nc.vector.tensor_copy(out=wr_sc[:], in_=wr_sc_raw[:].rearrange("p (m t) -> p t m", t=4))
 
-        def weave_views(dst, src):
-            return dst.rearrange("p (c i) t -> p c t i", i=2), src.rearrange("p t (c i) -> p c t i", i=2)
-
         rq_codes = {}
         rq_sc = {}
 
-        def prep_rq(h):
-            grouped = sb("rq_bf%d" % h, [P, PASSES, JH, 4], BF16, tag="late_page%d" % h)
+        def side_by_side(dst, src):
+            return dst.rearrange("p (c e) i -> p c i e", e=2), src.rearrange("p i (c e) -> p c i e", e=2)
+
+        def quantise_rq(h):
+            grouped = sb("rq_bf%d" % h, [P, PASSES, JH, 4], BF16)
             rq_codes[h] = sb("rq_codes%d" % h, [P, PASSES, JH], I32)
             rq_sc[h] = sb("rq_sc%d" % h, [P, PASSES, JH], U8)
             for z in range(PASSES):
-                if h == 0 and z == 1:
-                    cut = 192
-                    dst, src = weave_views(grouped[:, z, :cut], rq_raw[h, z][:, :, :cut])
+                cut = RQ_ON_VECTOR if (h, z) == (0, 1) else 0
+                if cut > 0:
+                    dst, src = side_by_side(grouped[:, z, :cut], rq_raw[h, z][:, :, :cut])
                     nc.vector.tensor_copy(out=dst, in_=src)
-                    dst, src = weave_views(grouped[:, z, cut:], rq_raw[h, z][:, :, cut:])
-                else:
-                    dst, src = weave_views(grouped[:, z], rq_raw[h, z][:])
+                dst, src = side_by_side(grouped[:, z, cut:], rq_raw[h, z][:, :, cut:])
                 nc.scalar.activation(dst, src, ACT.Copy)
                 nc.vector.quantize_mx(out=rq_codes[h][:, z, :].bitcast(FP8X4), scales=rq_sc[h][:, z, :], in_=grouped[:, z].rearrange("p j i -> p (j i)"))
 
-        def p_group(acc, t, h):
+        def p_product(acc, t, h):
             for z in range(PASSES):
-                nc.tensor.matmul_mx(out=acc[:, JH * h : JH * (h + 1)], lhsT=wr_half[t // 2][:, z, t % 2, :].bitcast(FP8X4), lhsT_scale=wr_sc[4 * z : P, t, :],
+                nc.tensor.matmul_mx(out=acc[:, JH * h : JH * (h + 1)], lhsT=wr[t // 2][:, z, t % 2, :].bitcast(FP8X4), lhsT_scale=wr_sc[4 * z : P, t, :],
                                     rhs=rq_codes[h][:, z, :].bitcast(FP8X4), rhs_scale=rq_sc[h][:, z, :], start=(z == 0), stop=(z == PASSES - 1))
 
         def patch_half(acc, t, h):
-            p_group(acc, t, h)
+            p_product(acc, t, h)
             pf = sb("pf%d%d" % (t, h), [P, JH], F32)
-            nc.scalar.activation(pf[:], acc[:, JH * h : JH * (h + 1)], ACT.Copy, scale=(gm_t if h == 0 else gm_raw)[:, t : t + 1])
+            nc.scalar.activation(pf[:], acc[:, JH * h : JH * (h + 1)], ACT.Copy, scale=(gm_first if h == 0 else gm_dealt)[:, t : t + 1])
             nc.vector.tensor_copy(pages[t][:].indirect(offsets[:, JH // 16 * h : JH // 16 * (h + 1)]), pf[:])
 
-        def make_pf(acc, t):
+        def whole_pf(acc, t):
             for h in range(2):
-                p_group(acc, t, h)
+                p_product(acc, t, h)
             pf = sb("pf%d" % t, [P, J], F32)
-            nc.scalar.activation(pf[:], acc[:], ACT.Copy, scale=gm_raw[:, t : t + 1])
+            nc.scalar.activation(pf[:], acc[:], ACT.Copy, scale=gm_dealt[:, t : t + 1])
             return pf
 
-        def scatter_whole(pf, t):
-            nc.vector.tensor_copy(pages[t][:].indirect(offsets[:]), pf[:])
+        def scatter_whole(t):
+            nc.vector.tensor_copy(pages[t][:].indirect(offsets[:]), pf_late[t][:])
 
-        prep_rq(0)
-        wr_half = []
-        for u in range(2):
-            wr_half.append(sb("wr%d" % u, [P, PASSES, 2, P], I32))
-            nc.vector.tensor_copy(out=wr_half[u][:].rearrange("p z t m -> p z m t"), in_=wr_raw[:].rearrange("p z (m t) -> p z m t", t=4)[:, :, :, 2 * u : 2 * u + 2])
+        quantise_rq(0)
+        wr = []
+        for pair in range(2):
+            wr.append(sb("wr%d" % pair, [P, PASSES, 2, P], I32))
+            nc.vector.tensor_copy(out=wr[pair][:].rearrange("p z t m -> p z m t"), in_=wr_raw[:].rearrange("p z (m t) -> p z m t", t=4)[:, :, :, 2 * pair : 2 * pair + 2])
         xq_sc = sb("xq_sc", [P, PASSES, T], U8, tag="wr_raw")
         nc.vector.memset(xq_sc[:].bitcast(I32), 0)
-        for r in range(4):
-            nc.sync.dma_start(out=xq_sc[r:P:32, :, :].bitcast(I32), in_=xq_scales.rearrange("z (q r) c -> r q z c", r=4)[r].bitcast(I32))
+        load_plane(nc.sync, xq_sc, xq_scales)
         p_acc = {t: bank(t, "p%d" % t) for t in (0, 1)}
         for t in (0, 1):
             patch_half(p_acc[t], t, 0)
-        prep_rq(1)
-        wa = deal_words("wa", wa_raw, tag="late_page1")
+        quantise_rq(1)
+        wa = sb("wa", [P, PASSES, 4, P], I32, tag="rq_bf1")
+        nc.vector.tensor_copy(out=wa[:].rearrange("p z t m -> p z m t"), in_=wa_raw[:].rearrange("p z (m t) -> p z m t", t=4))
         wa_sc = sb("wa_sc", [P, PASSES, 4, P], U8, tag="rq_raw11")
         nc.vector.tensor_copy(out=wa_sc[:], in_=wa_sc_raw[:].rearrange("p z (m t) -> p z t m", t=4))
         for t in (0, 1):
             patch_half(p_acc[t], t, 1)
-        pf_late = {t: make_pf(bank(t, "p%d" % t), t) for t in (2, 3)}
+        pf_late = {t: whole_pf(bank(t, "p%d" % t), t) for t in (2, 3)}
 
-        def z_group(b, t, c):
-            acc = bank(b, "z%d%d" % (t, c))
+        z_banks = ((4, 5, 6, 7), (0, 1, 2, 3), (4, 0, 3, 1), (3, 2, 5, 6))
+        rows_of = out_0.rearrange("(p t) c -> t p c", t=4)
+        words_out = out_1[0].rearrange("p c r -> p (c r)").bitcast(I32)
+        s = {(pair, c): sb("s%d%d" % (pair, c), [P, 2, CH], F32) for pair in range(2) for c in range(NCH)}
+        y_bf = [sb("y_bf%d" % c, [P, CH, 4], BF16) for c in range(NCH)]
+        y_sc = sb("y_sc", [P, T], U8)
+        z_sb = {}
+
+        def z_product(t, c):
+            acc = bank(z_banks[t][c], "z%d%d" % (t, c))
             for z in range(PASSES):
                 nc.tensor.matmul_mx(out=acc[:], lhsT=wa[:, z, t, :].bitcast(FP8X4), lhsT_scale=wa_sc[:, z, t, :],
                                     rhs=xq[c][:, z, :].bitcast(FP4X4), rhs_scale=xq_sc[:, z, CH * c : CH * (c + 1)], start=(z == 0), stop=(z == PASSES - 1))
             return acc
 
-        rows_of = out_0.rearrange("(p t) c -> t p c", t=4)
-
-        s = {(pair, c): sb("s%d%d" % (pair, c), [P, 2, CH], F32) for pair in range(2) for c in range(NCH)}
-        y_bf = [sb("y_bf%d" % c, [P, CH, 4], BF16) for c in range(NCH)]
-        y_sc = sb("y_sc", [P, T], U8)
-        words_out = out_1[0].rearrange("p c r -> p (c r)")
-        z_banks = ((4, 5, 6, 7), (0, 1, 2, 3), (4, 0, 1, 2), (3, 5, 6, 7))
+        def z_to_sbuf(t, c):
+            z_sb[t, c] = sb("z_sb%d%d" % (t, c), [P, CH], F32)
+            nc.scalar.copy(z_sb[t, c][:], z_product(t, c)[:])
 
         def add(t, c):
-            acc = z_group(z_banks[t][c], t, c)
-            nc.vector.tensor_tensor(s[t // 2, c][:, t % 2, :], acc[:], pages[t][:, CH * c : CH * (c + 1)], ALU.add)
+            dst, page = s[t // 2, c][:, t % 2, :], pages[t][:, CH * c : CH * (c + 1)]
+            if (t, c) in z_sb:
+                nc.gpsimd.tensor_tensor(dst, z_sb[t, c][:], page, ALU.add)
+            else:
+                nc.vector.tensor_tensor(dst, z_product(t, c)[:], page, ALU.add)
 
-        def relu(t, c):
+        def relu(t, c, engine, y):
+            src = s[t // 2, c][:, t % 2, :]
+            if engine == SCALAR:
+                nc.scalar.activation(y, src, ACT.Relu)
+            else:
+                nc.gpsimd.tensor_scalar(y, src, F32_MAX, 0.0, ALU.min, ALU.max)
+
+        def store(t, c, y):
+            nc.sync.dma_start(out=rows_of[t][:, CH * c : CH * c + y.shape[1]], in_=y)
+
+        def relu_store(t, c, engine):
             y = sb("y%d%d" % (t, c), [P, CH], F32)
-            nc.scalar.activation(y[:], s[t // 2, c][:, t % 2, :], ACT.Relu)
-            nc.sync.dma_start(out=rows_of[t][:, CH * c : CH * (c + 1)], in_=y[:])
+            relu(t, c, engine, y[:])
+            store(t, c, y[:])
 
-        pairs = [sb("pairs%d" % c, [P, 2, CH, 2], BF16) for c in range(NCH)]
+        def add_relu_store(t, c, engine):
+            add(t, c)
+            relu_store(t, c, engine)
 
-        def merge(c):
-            nc.vector.tensor_copy(out=y_bf[c][:].bitcast(I32), in_=pairs[c][:].rearrange("p u c t -> p u (c t)").bitcast(I32).rearrange("p u c -> p c u"))
-
-        def weave(pair, c, on_scalar, lo=0, hi=CH):
-            dst, src = pairs[c][:, pair, lo:hi, :], s[pair, c][:, :, lo:hi].rearrange("p t c -> p c t")
-            if on_scalar:
+        def weave(pair, c, engine, lo=0, hi=CH):
+            dst, src = y_bf[c][:, lo:hi, 2 * pair : 2 * pair + 2], s[pair, c][:, :, lo:hi].rearrange("p t c -> p c t")
+            if engine == SCALAR:
                 nc.scalar.activation(dst, src, ACT.Relu)
             else:
                 nc.vector.tensor_scalar_max(dst, src, 0.0)
 
         def planes(c):
-            nc.vector.quantize_mx(out=codes[:, CH * c : CH * (c + 1)].bitcast(FP8X4), scales=y_sc[:, CH * c : CH * (c + 1)], in_=y_bf[c][:].rearrange("p c t -> p (c t)"))
-            nc.sync.dma_start(out=words_out[:, 4 * CH * c : 4 * CH * (c + 1)].bitcast(I32), in_=codes[:, CH * c : CH * (c + 1)])
+            cols = slice(CH * c, CH * (c + 1))
+            nc.vector.quantize_mx(out=codes[:, cols].bitcast(FP8X4), scales=y_sc[:, cols], in_=y_bf[c][:].rearrange("p c t -> p (c t)"))
+            nc.sync.dma_start(out=words_out[:, cols], in_=codes[:, cols])
 
-        def both(t, c):
-            add(t, c)
-            relu(t, c)
+        add(0, 0)
+        z_to_sbuf(1, 3)
+        z_to_sbuf(2, 2)
+        add(1, 3)
+        relu_store(0, 0, GPSIMD)
+        add_relu_store(1, 0, GPSIMD)
+        weave(0, 0, SCALAR)
+        add_relu_store(1, 1, SCALAR)
+        add_relu_store(1, 2, SCALAR)
+        relu_store(1, 3, SCALAR)
+        add_relu_store(0, 1, SCALAR)
+        weave(0, 1, SCALAR)
+        scatter_whole(2)
 
-        both(0, 0)
-        both(1, 0)
-        weave(0, 0, True)
-        for c in (1, 2, 3):
-            both(1, c)
-        both(0, 1)
-        weave(0, 1, True)
-        scatter_whole(pf_late[2], 2)
-        both(0, 2)
-        weave(0, 2, True)
-        both(2, 0)
-        both(2, 1)
-        both(0, 3)
-        weave(0, 3, True)
-        both(2, 2)
-        codes = sb("codes", [P, T], I32, tag="y22")
-        scatter_whole(pf_late[3], 3)
-        both(2, 3)
-        for c in range(NCH):
+        add_relu_store(2, 2, GPSIMD)
+        add_relu_store(0, 2, SCALAR)
+        add_relu_store(2, 0, SCALAR)
+        weave(0, 2, SCALAR)
+        add(2, 1)
+        add_relu_store(0, 3, SCALAR)
+        weave(0, 3, SCALAR)
+        relu_store(2, 1, SCALAR)
+        scatter_whole(3)
+
+        codes = sb("codes", [P, T], I32, tag="y03")
+        y_gpsimd = sb("y_gpsimd", [P, 3 * CH], F32, tag="s03")
+        y_scalar = sb("y_scalar", [P, 2 * CH], F32)
+        add(2, 3)
+        relu(2, 3, GPSIMD, y_gpsimd[:, :CH])
+        store(2, 3, y_gpsimd[:, :CH])
+        for c in (0, 1):
             add(3, c)
-        weave(1, 0, True)
-        weave(1, 1, True)
-        weave(1, 3, False, CH // 2, CH)
-        relu(3, 0)
-        weave(1, 2, True)
-        weave(1, 3, True, 0, CH // 2)
-        merge(0)
-        merge(1)
+            relu(3, c, GPSIMD, y_gpsimd[:, CH * (c + 1) : CH * (c + 2)])
+        store(3, 0, y_gpsimd[:, CH:])
+        weave(1, 0, SCALAR)
+        add(3, 2)
+        add(3, 3)
+        weave(1, 2, SCALAR)
+        weave(1, 1, VECTOR)
         planes(0)
-        relu(3, 1)
-        merge(2)
+        weave(1, 3, SCALAR, 0, CH // 2)
+        weave(1, 3, VECTOR, CH // 2, CH)
         planes(1)
-        relu(3, 2)
-        merge(3)
+        relu(3, 2, SCALAR, y_scalar[:, :CH])
         planes(2)
-        relu(3, 3)
+        relu(3, 3, SCALAR, y_scalar[:, CH:])
+        store(3, 2, y_scalar[:])
         planes(3)
         for r in range(4):
             queue = nc.scalar if r % 2 == 0 else nc.sync

from contextlib import ExitStack

import concourse.mybir as mybir

K, T, J, N = 1024, 2048, 512, 512
FLOPS = 2 * K * N * (T + J)

F32 = mybir.dt.float32
BF16 = mybir.dt.bfloat16
I32 = mybir.dt.int32
U16 = mybir.dt.uint16
U8 = mybir.dt.uint8
FP8X4 = mybir.dt.float8_e4m3fn_x4
FP4X4 = mybir.dt.float4_e2m1fn_x4
ALU = mybir.AluOpType
ACT = mybir.ActivationFunctionType

P = 128
PASSES = 2
CH = 512
NCH = T // CH
JH = J // 2
RQ_ON_VECTOR = 192
F32_MAX = 3.4028234663852886e38
SCALAR, VECTOR, GPSIMD = "scalar", "vector", "gpsimd"


def tile_list_head_patches_pl_kernel(tc, xq_words, xq_scales, wa_words, wa_scales, rq, wr_words, wr_scales, gm, offs, out_0, out_1, out_2):
    nc = tc.nc
    with ExitStack() as ctx:
        keep = ctx.enter_context(tc.tile_pool(name="keep", bufs=1))
        psum = ctx.enter_context(tc.psum_pool(name="psum", bufs=1))

        def sb(name, shape, dtype, tag=None):
            return keep.tile(shape, dtype, name=name, tag=tag or name, align_bytes=64)

        def bank(b, name):
            return psum.tile([P, CH], F32, name=name, tag="bank%d" % b)

        offsets = keep.tile([P, J // 16], U16, name="offsets")
        wr_sc_raw = sb("wr_sc_raw", [P, N], U8)
        wa_sc_raw = sb("wa_sc_raw", [P, PASSES, N], U8)
        nc.vector.memset(wr_sc_raw[:].bitcast(I32), 0)
        nc.vector.memset(wa_sc_raw[:].bitcast(I32), 0)
        page_a = sb("page_a", [P, T], F32)
        page_b = sb("page_b", [P, T], F32)
        nc.vector.memset(page_a[:].bitcast(I32), 0)
        nc.vector.memset(page_b[:].bitcast(I32), 0)
        pages = (page_a, page_b, page_b, page_a)

        rq_raw = {}

        def load_rq(h, z):
            rq_raw[h, z] = sb("rq_raw%d%d" % (h, z), [P, 4, JH], F32)
            rows = rq[512 * z : 512 * (z + 1), :].rearrange("(p i) j -> p i j", i=4)
            nc.sync.dma_start(out=rq_raw[h, z][:], in_=rows[:, :, JH * h : JH * (h + 1)])

        def load_words(name, words):
            raw = sb(name, [P, PASSES, N], I32)
            nc.sync.dma_start(out=raw[:], in_=words.rearrange("z p n r -> p z (n r)").bitcast(I32))
            return raw

        def load_plane(queue, plane, scales):
            for r in range(4):
                queue.dma_start(out=plane[r:P:32, :, :].bitcast(I32), in_=scales.rearrange("z (q r) c -> r q z c", r=4)[r].bitcast(I32))

        load_rq(0, 0)
        for q in range(4):
            nc.scalar.dma_start(out=wr_sc_raw[32 * q : 32 * q + 8, :].bitcast(I32), in_=wr_scales[:, 4 * q : 4 * q + 4, :].bitcast(I32))
        load_rq(0, 1)
        wr_raw = load_words("wr_raw", wr_words)
        gm_dealt = sb("gm_dealt", [P, 4], F32)
        nc.sync.dma_start(out=gm_dealt[:], in_=gm.rearrange("(p t) o -> p (t o)", t=4))
        nc.sync.dma_start(offsets[:], offs)
        load_rq(1, 0)
        load_rq(1, 1)
        load_plane(nc.gpsimd, wa_sc_raw, wa_scales)
        wa_raw = load_words("wa_raw", wa_words)
        xq = []
        for c in range(NCH):
            xq.append(sb("xq%d" % c, [P, PASSES, 2 * CH], U8))
            nc.sync.dma_start(out=xq[c][:].bitcast(I32), in_=xq_words.rearrange("z p b -> p z b")[:, :, 2 * CH * c : 2 * CH * (c + 1)].bitcast(I32))

        gm_first = sb("gm_first", [P, 4], F32, tag="rq_bf1")
        nc.scalar.activation(gm_first[:], gm_dealt[:], ACT.Copy)

        wr_sc = sb("wr_sc", [P, 4, P], U8)
        nc.vector.tensor_copy(out=wr_sc[:], in_=wr_sc_raw[:].rearrange("p (m t) -> p t m", t=4))

        rq_codes = {}
        rq_sc = {}

        def side_by_side(dst, src):
            return dst.rearrange("p (c e) i -> p c i e", e=2), src.rearrange("p i (c e) -> p c i e", e=2)

        def quantise_rq(h):
            grouped = sb("rq_bf%d" % h, [P, PASSES, JH, 4], BF16)
            rq_codes[h] = sb("rq_codes%d" % h, [P, PASSES, JH], I32)
            rq_sc[h] = sb("rq_sc%d" % h, [P, PASSES, JH], U8)
            for z in range(PASSES):
                cut = RQ_ON_VECTOR if (h, z) == (0, 1) else 0
                if cut > 0:
                    dst, src = side_by_side(grouped[:, z, :cut], rq_raw[h, z][:, :, :cut])
                    nc.vector.tensor_copy(out=dst, in_=src)
                dst, src = side_by_side(grouped[:, z, cut:], rq_raw[h, z][:, :, cut:])
                nc.scalar.activation(dst, src, ACT.Copy)
                nc.vector.quantize_mx(out=rq_codes[h][:, z, :].bitcast(FP8X4), scales=rq_sc[h][:, z, :], in_=grouped[:, z].rearrange("p j i -> p (j i)"))

        def p_product(acc, t, h):
            for z in range(PASSES):
                nc.tensor.matmul_mx(out=acc[:, JH * h : JH * (h + 1)], lhsT=wr[t // 2][:, z, t % 2, :].bitcast(FP8X4), lhsT_scale=wr_sc[4 * z : P, t, :],
                                    rhs=rq_codes[h][:, z, :].bitcast(FP8X4), rhs_scale=rq_sc[h][:, z, :], start=(z == 0), stop=(z == PASSES - 1))

        def patch_half(acc, t, h):
            p_product(acc, t, h)
            pf = sb("pf%d%d" % (t, h), [P, JH], F32)
            nc.scalar.activation(pf[:], acc[:, JH * h : JH * (h + 1)], ACT.Copy, scale=(gm_first if h == 0 else gm_dealt)[:, t : t + 1])
            nc.vector.tensor_copy(pages[t][:].indirect(offsets[:, JH // 16 * h : JH // 16 * (h + 1)]), pf[:])

        def whole_pf(acc, t):
            for h in range(2):
                p_product(acc, t, h)
            pf = sb("pf%d" % t, [P, J], F32)
            nc.scalar.activation(pf[:], acc[:], ACT.Copy, scale=gm_dealt[:, t : t + 1])
            return pf

        def scatter_whole(t):
            nc.vector.tensor_copy(pages[t][:].indirect(offsets[:]), pf_late[t][:])

        quantise_rq(0)
        wr = []
        for pair in range(2):
            wr.append(sb("wr%d" % pair, [P, PASSES, 2, P], I32))
            nc.vector.tensor_copy(out=wr[pair][:].rearrange("p z t m -> p z m t"), in_=wr_raw[:].rearrange("p z (m t) -> p z m t", t=4)[:, :, :, 2 * pair : 2 * pair + 2])
        xq_sc = sb("xq_sc", [P, PASSES, T], U8, tag="wr_raw")
        nc.vector.memset(xq_sc[:].bitcast(I32), 0)
        load_plane(nc.sync, xq_sc, xq_scales)
        p_acc = {t: bank(t, "p%d" % t) for t in (0, 1)}
        for t in (0, 1):
            patch_half(p_acc[t], t, 0)
        quantise_rq(1)
        wa = sb("wa", [P, PASSES, 4, P], I32, tag="rq_bf1")
        nc.vector.tensor_copy(out=wa[:].rearrange("p z t m -> p z m t"), in_=wa_raw[:].rearrange("p z (m t) -> p z m t", t=4))
        wa_sc = sb("wa_sc", [P, PASSES, 4, P], U8, tag="rq_raw11")
        nc.vector.tensor_copy(out=wa_sc[:], in_=wa_sc_raw[:].rearrange("p z (m t) -> p z t m", t=4))
        for t in (0, 1):
            patch_half(p_acc[t], t, 1)
        pf_late = {t: whole_pf(bank(t, "p%d" % t), t) for t in (2, 3)}

        z_banks = ((4, 5, 6, 7), (0, 1, 2, 3), (4, 0, 3, 1), (3, 2, 5, 6))
        rows_of = out_0.rearrange("(p t) c -> t p c", t=4)
        words_out = out_1[0].rearrange("p c r -> p (c r)").bitcast(I32)
        s = {(pair, c): sb("s%d%d" % (pair, c), [P, 2, CH], F32) for pair in range(2) for c in range(NCH)}
        y_bf = [sb("y_bf%d" % c, [P, CH, 4], BF16) for c in range(NCH)]
        y_sc = sb("y_sc", [P, T], U8)
        z_sb = {}

        def z_product(t, c):
            acc = bank(z_banks[t][c], "z%d%d" % (t, c))
            for z in range(PASSES):
                nc.tensor.matmul_mx(out=acc[:], lhsT=wa[:, z, t, :].bitcast(FP8X4), lhsT_scale=wa_sc[:, z, t, :],
                                    rhs=xq[c][:, z, :].bitcast(FP4X4), rhs_scale=xq_sc[:, z, CH * c : CH * (c + 1)], start=(z == 0), stop=(z == PASSES - 1))
            return acc

        def z_to_sbuf(t, c):
            z_sb[t, c] = sb("z_sb%d%d" % (t, c), [P, CH], F32)
            nc.scalar.copy(z_sb[t, c][:], z_product(t, c)[:])

        def add(t, c):
            dst, page = s[t // 2, c][:, t % 2, :], pages[t][:, CH * c : CH * (c + 1)]
            if (t, c) in z_sb:
                nc.gpsimd.tensor_tensor(dst, z_sb[t, c][:], page, ALU.add)
            else:
                nc.vector.tensor_tensor(dst, z_product(t, c)[:], page, ALU.add)

        def relu(t, c, engine, y):
            src = s[t // 2, c][:, t % 2, :]
            if engine == SCALAR:
                nc.scalar.activation(y, src, ACT.Relu)
            else:
                nc.gpsimd.tensor_scalar(y, src, F32_MAX, 0.0, ALU.min, ALU.max)

        def store(t, c, y):
            nc.sync.dma_start(out=rows_of[t][:, CH * c : CH * c + y.shape[1]], in_=y)

        def relu_store(t, c, engine):
            y = sb("y%d%d" % (t, c), [P, CH], F32)
            relu(t, c, engine, y[:])
            store(t, c, y[:])

        def add_relu_store(t, c, engine):
            add(t, c)
            relu_store(t, c, engine)

        def weave(pair, c, engine, lo=0, hi=CH):
            dst, src = y_bf[c][:, lo:hi, 2 * pair : 2 * pair + 2], s[pair, c][:, :, lo:hi].rearrange("p t c -> p c t")
            if engine == SCALAR:
                nc.scalar.activation(dst, src, ACT.Relu)
            else:
                nc.vector.tensor_scalar_max(dst, src, 0.0)

        def planes(c):
            cols = slice(CH * c, CH * (c + 1))
            nc.vector.quantize_mx(out=codes[:, cols].bitcast(FP8X4), scales=y_sc[:, cols], in_=y_bf[c][:].rearrange("p c t -> p (c t)"))
            nc.sync.dma_start(out=words_out[:, cols], in_=codes[:, cols])

        add(0, 0)
        z_to_sbuf(1, 3)
        z_to_sbuf(2, 2)
        add(1, 3)
        relu_store(0, 0, GPSIMD)
        add_relu_store(1, 0, GPSIMD)
        weave(0, 0, SCALAR)
        add_relu_store(1, 1, SCALAR)
        add_relu_store(1, 2, SCALAR)
        relu_store(1, 3, SCALAR)
        add_relu_store(0, 1, SCALAR)
        weave(0, 1, SCALAR)
        scatter_whole(2)

        add_relu_store(2, 2, GPSIMD)
        add_relu_store(0, 2, SCALAR)
        add_relu_store(2, 0, SCALAR)
        weave(0, 2, SCALAR)
        add(2, 1)
        add_relu_store(0, 3, SCALAR)
        weave(0, 3, SCALAR)
        relu_store(2, 1, SCALAR)
        scatter_whole(3)

        codes = sb("codes", [P, T], I32, tag="y03")
        y_gpsimd = sb("y_gpsimd", [P, 3 * CH], F32, tag="s03")
        y_scalar = sb("y_scalar", [P, 2 * CH], F32)
        add(2, 3)
        relu(2, 3, GPSIMD, y_gpsimd[:, :CH])
        store(2, 3, y_gpsimd[:, :CH])
        for c in (0, 1):
            add(3, c)
            relu(3, c, GPSIMD, y_gpsimd[:, CH * (c + 1) : CH * (c + 2)])
        store(3, 0, y_gpsimd[:, CH:])
        weave(1, 0, SCALAR)
        add(3, 2)
        add(3, 3)
        weave(1, 2, SCALAR)
        weave(1, 1, VECTOR)
        planes(0)
        weave(1, 3, SCALAR, 0, CH // 2)
        weave(1, 3, VECTOR, CH // 2, CH)
        planes(1)
        relu(3, 2, SCALAR, y_scalar[:, :CH])
        planes(2)
        relu(3, 3, SCALAR, y_scalar[:, CH:])
        store(3, 2, y_scalar[:])
        planes(3)
        for r in range(4):
            queue = nc.scalar if r % 2 == 0 else nc.sync
            queue.dma_start(out=out_2[0].rearrange("(q r) c -> r q c", r=4)[r].bitcast(I32), in_=y_sc[r:P:32, :].bitcast(I32))
